import numpy as np
import ml_dtypes


def mxq(x, axis, fmt="e4m3"):
    dtype, down = {"e4m3": (ml_dtypes.float8_e4m3fn, 7), "e5m2": (ml_dtypes.float8_e5m2, 14)}[fmt]
    v = np.moveaxis(np.asarray(x, np.float32).astype(ml_dtypes.bfloat16).astype(np.float64), axis, -1)
    blocks = v.reshape(v.shape[:-1] + (-1, 32))
    amax = np.abs(blocks).max(-1, keepdims=True)
    byte = np.maximum(np.where(amax > 0, np.frexp(amax)[1] - 1 + 127, 0) - down, 1)
    scale = np.exp2(byte - 127.0)
    codes = (blocks / scale).astype(np.float32).astype(dtype).astype(np.float64)
    return np.moveaxis((codes * scale).reshape(v.shape), -1, axis)


WIDE = False


def mx_kscale(k):
    if not WIDE:
        return np.ones(k)
    levels = np.array([30, -30])
    if k % 512:
        return np.exp2(np.random.permutation(np.resize(levels, k // 32))).repeat(32)
    a = np.empty((k // 512, 16))
    for p in range(k // 512):
        a[p, :8] = np.random.permutation(np.resize(levels, 8))
        for g in range(8):
            far = levels[np.abs(levels - a[p, g]) >= 10]
            a[p, g + 8] = far[np.random.randint(len(far))]
    return np.exp2(a.ravel()).repeat(32)


def f64(x):
    return np.asarray(x).astype(np.float64)


def striped(idx):
    return np.tile(np.asarray(idx).reshape(-1, 16).T, (8, 1)).astype(np.uint16)


def unstriped(offs):
    return offs[:16].T.reshape(-1).astype(np.int64)


E2M1 = np.array([0.0, 0.5, 1.0, 1.5, 2.0, 3.0, 4.0, 6.0, -0.0, -0.5, -1.0, -1.5, -2.0, -3.0, -4.0, -6.0])


def pack_weight(w, fmt):
    k, n = w.shape
    w = f64(np.asarray(w, np.float32).astype(ml_dtypes.bfloat16)).reshape(k // 32, 32, n)
    amax = np.abs(w).max(1)
    if fmt == "e4m3":
        byte = np.frexp(amax)[1] - 1 + 127 - 7
    else:
        mant, ex = np.frexp(amax / 6.0)
        byte = np.where(mant > 0.5, ex, ex - 1) + 127
    byte = np.clip(np.where(amax > 0, byte, 1), 1, 254)
    scaled = (w * np.exp2(127.0 - byte)[:, None, :]).reshape(k, n).astype(np.float32)
    by_word = np.ascontiguousarray(scaled.reshape(k // 512, 128, 4, n).transpose(0, 1, 3, 2))
    if fmt == "e4m3":
        words = by_word.astype(ml_dtypes.float8_e4m3fn).view(np.uint8)
    else:
        c = by_word.astype(ml_dtypes.float4_e2m1fn).view(np.uint8) & 0xF
        words = (c[..., 0::2] | (c[..., 1::2] << 4)).reshape(k // 512, 128, 2 * n)
    return np.ascontiguousarray(words), np.ascontiguousarray(byte.astype(np.uint8).reshape(k // 512, 16, n))


def unpack_weight(words, scales, fmt):
    g, _, n = scales.shape
    words = np.ascontiguousarray(words).reshape(g, 128, n, -1)
    if fmt == "e4m3":
        vals = words.view(ml_dtypes.float8_e4m3fn).astype(np.float64)
    else:
        nib = np.empty((g, 128, n, 4), np.uint8)
        nib[..., 0::2] = words & 0xF
        nib[..., 1::2] = words >> 4
        vals = E2M1[nib]
    vals = vals * np.repeat(np.exp2(scales.astype(np.float64) - 127.0), 8, axis=1)[..., None]
    return vals.transpose(0, 1, 3, 2).reshape(g * 512, n)


K, J, N, R, T, V, Q = 512, 512, 256, 256, 1024, 1024, 64


def setup_inputs():
    n = np.random.standard_normal
    idx = np.random.permutation(T)[:J]
    idx2 = np.random.permutation(T)[:J]
    idx3 = np.random.permutation(V)[:J]
    idx4 = np.random.permutation(V)[:J]
    fj = mx_kscale(J)
    fk = mx_kscale(K)
    drp = pack_weight(n((K, R)) * 1 / np.sqrt(K) / fk[:, None], "e4m3")
    return {
        "xf": (n((K, T))).astype(np.float32),
        "ra": (np.random.uniform(0.5, 1.5, (1, J)) * fj).astype(np.float32),
        "gt": (n((N, V)) * np.exp(0.5 * n((1, V)))).astype(np.float32),
        "rb": (np.random.uniform(0.5, 1.5, (1, J)) / fj).astype(np.float32),
        "fkr": (np.random.uniform(0.5, 1.5, (1, K)) * fk).astype(np.float32),
        "dr_words": drp[0],
        "dr_scales": drp[1],
        "gr1c": (np.random.uniform(0.5, 2.0, (R, 1))).astype(np.float32),
        "offs": striped(idx),
        "offs2": striped(idx2),
        "offs3": striped(idx3),
        "offs4": striped(idx4),
    }


def reference(xf, ra, gt, rb, fkr, dr_words, dr_scales, gr1c, offs, offs2, offs3, offs4):
    idx = unstriped(offs)
    idx2 = unstriped(offs2)
    idx3 = unstriped(offs3)
    idx4 = unstriped(offs4)
    dru = unpack_weight(dr_words, dr_scales, "e4m3")
    us = (f64(xf)[:, idx] - f64(xf)[:, idx2]) * f64(ra)
    ut = us.T
    uj = ut * f64(fkr)
    gs = (f64(gt)[:, idx3] - 0.7 * f64(gt)[:, idx4]) * f64(rb)
    gj = gs.T
    ujq = mxq(uj, 0, "e4m3")
    gjq = mxq(gj, 0, "e5m2")
    w = ujq.T @ gjq
    wq = mxq(w, 0, "e5m2")
    v2 = dru.T @ wq
    wq = v2.reshape(R, Q, N // Q).sum(axis=2)
    y = 0.02 * wq * f64(gr1c)
    return y

@@ -1,0 +1,241 @@
+from contextlib import ExitStack
+
+import concourse.mybir as mybir
+from concourse.masks import make_identity
+
+K, J, N, R, T, V, Q = 512, 512, 256, 256, 1024, 1024, 64
+FLOPS = 2 * J * K * N + 2 * K * R * N
+
+F32 = mybir.dt.float32
+BF16 = mybir.dt.bfloat16
+I32 = mybir.dt.int32
+U32 = mybir.dt.uint32
+U16 = mybir.dt.uint16
+U8 = mybir.dt.uint8
+E4M3 = mybir.dt.float8_e4m3fn_x4
+E5M2 = mybir.dt.float8_e5m2_x4
+MULT = mybir.AluOpType.mult
+ADD = mybir.AluOpType.add
+SUB = mybir.AluOpType.subtract
+COPY = mybir.ActivationFunctionType.Copy
+
+P = 128
+PACK = 4
+
+
+def tile_list_directions_gaps_differences_sums_kernel(
+    tc, xf, ra, gt, rb, fkr, dr_words, dr_scales, gr1c, offs, offs2, offs3, offs4, out
+):
+    nc = tc.nc
+    with ExitStack() as ctx:
+        keep = ctx.enter_context(tc.tile_pool(name="keep", bufs=1))
+        psum = ctx.enter_context(tc.psum_pool(name="psum", bufs=1))
+
+        lists = [keep.tile([P, J // 16], U16, name=f"list{i}") for i in range(4)]
+        x_rows = xf.rearrange("(p a) t -> p a t", a=PACK)
+        g_rows = gt.rearrange("(p b) v -> p b v", b=2)
+        x_win = [keep.tile([P, T], F32, name=f"x_win{a}") for a in range(PACK)]
+        g_win = [keep.tile([P, V], F32, name=f"g_win{b}") for b in range(2)]
+        ra_col = keep.tile([P, PACK], F32)
+        rb_col = keep.tile([P, PACK], F32)
+        fk_col = keep.tile([P, PACK], F32)
+        gr_col = keep.tile([P, 2], F32)
+        dr_codes = keep.tile([P, R], U32, align_bytes=64)
+        dr_plane = keep.tile([P, R], U8, align_bytes=64)
+        ident = keep.tile([P, P], F32)
+
+        nc.sync.dma_start(out=g_win[0][:], in_=g_rows[:, 0, :])
+        nc.sync.dma_start(lists[2][:], offs3)
+        nc.sync.dma_start(lists[3][:], offs4)
+        nc.sync.dma_start(out=x_win[0][:], in_=x_rows[:, 0, :])
+        nc.sync.dma_start(lists[1][:], offs2)
+        nc.sync.dma_start(lists[0][:], offs)
+        nc.scalar.dma_start(out=ra_col[:], in_=ra.rearrange("o (p t) -> p (o t)", t=PACK))
+        nc.scalar.dma_start(out=fk_col[:], in_=fkr.rearrange("o (p a) -> p (o a)", a=PACK))
+        nc.sync.dma_start(out=x_win[1][:], in_=x_rows[:, 1, :])
+        nc.sync.dma_start(out=rb_col[:], in_=rb.rearrange("o (p t) -> p (o t)", t=PACK))
+        nc.sync.dma_start(out=g_win[1][:], in_=g_rows[:, 1, :])
+        nc.sync.dma_start(out=x_win[2][:], in_=x_rows[:, 2, :])
+        nc.sync.dma_start(out=x_win[3][:], in_=x_rows[:, 3, :])
+        nc.sync.dma_start(
+            out=dr_codes[:].bitcast(I32), in_=dr_words[0].rearrange("p c t -> p (c t)").bitcast(I32)
+        )
+        nc.gpsimd.memset(dr_plane[:].bitcast(I32), 0)
+        for quad in range(4):
+            nc.sync.dma_start(
+                out=dr_plane[32 * quad : 32 * quad + 4, :].bitcast(I32),
+                in_=dr_scales[0, 4 * quad : 4 * quad + 4, :].bitcast(I32),
+            )
+        with nc.allow_non_contiguous_dma(reason="one factor a partition"):
+            nc.sync.dma_start(out=gr_col[:], in_=gr1c.rearrange("(h p) o -> p (h o)", p=P))
+
+        make_identity(nc, ident[:])
+
+        ra_all = psum.tile([P, PACK, P], F32)
+        for t in range(PACK):
+            nc.tensor.transpose(ra_all[:, t, :], ra_col[:, t : t + 1].to_broadcast([P, P]), ident[:])
+
+        HALF = J // 2
+        u_second, u_diff, u_round, u_bank, u_packed, u_codes, u_plane = {}, {}, {}, {}, {}, {}, {}
+        g_packed, g_codes, g_plane = {}, {}, {}
+        g_first = [keep.tile([P, J], F32, name=f"g_first{b}") for b in range(2)]
+        g_second = [keep.tile([P, J], F32, name=f"g_second{b}") for b in range(2)]
+        g_bank = [psum.tile([P, PACK, P], F32, name=f"g_bank{b}") for b in range(2)]
+        w_bank = [psum.tile([P, PACK, P], F32, name=f"w_bank{b}") for b in range(2)]
+
+        def g_gather_first_vector(b):
+            nc.vector.tensor_copy(g_first[b][:], g_win[b][:].indirect(lists[2][:]))
+
+        def g_gather_first_scalar(b):
+            nc.scalar.activation(g_first[b][:], g_win[b][:].indirect(lists[2][:]), COPY)
+
+        def g_gather_second(b):
+            nc.scalar.activation(g_second[b][:], g_win[b][:].indirect(lists[3][:]), COPY, scale=-0.7)
+
+        def g_turn(b):
+            for i, picked in enumerate((g_first[b], g_second[b])):
+                for t in range(PACK):
+                    nc.tensor.matmul(
+                        g_bank[b][:, t, :], picked[:, t:J:PACK], ident[:], is_transpose=True,
+                        start=(i == 0 and t == 0), stop=(i == 1 and t == PACK - 1),
+                    )
+
+        def g_pack(b, slot):
+            g_packed[b] = keep.tile([P, J], BF16, name=f"g_packed{b}", tag=slot, align_bytes=64)
+            nc.vector.tensor_tensor(
+                g_packed[b][:].rearrange("p (m t) -> p m t", t=PACK),
+                g_bank[b][:].rearrange("p t m -> p m t"),
+                rb_col[:].unsqueeze(1).to_broadcast([P, P, PACK]),
+                MULT,
+            )
+
+        def g_quantize(b):
+            g_codes[b] = keep.tile([P, P], U32, name=f"g_codes{b}", align_bytes=64)
+            g_plane[b] = keep.tile([P, P], U8, name=f"g_plane{b}", align_bytes=64)
+            nc.vector.quantize_mx(g_codes[b][:].bitcast(E5M2), g_plane[b][:], g_packed[b][:])
+
+        def u_gather_second(a):
+            for i in range(2):
+                u_second[a, i] = keep.tile([P, HALF], F32, name=f"u_second{a}{i}", align_bytes=64)
+                nc.scalar.activation(
+                    u_second[a, i][:], x_win[a][:].indirect(lists[1][:, i * 16 : (i + 1) * 16]), COPY
+                )
+
+        def u_gather_first(a):
+            for i in range(2):
+                u_diff[a, i] = keep.tile([P, HALF], F32, name=f"u_diff{a}{i}", align_bytes=64)
+                nc.vector.tensor_tensor(
+                    u_diff[a, i][:], x_win[a][:].indirect(lists[0][:, i * 16 : (i + 1) * 16]),
+                    u_second[a, i][:], SUB,
+                )
+
+        def u_scale(a):
+            u_round[a] = keep.tile([P, J], BF16, name=f"u_round{a}")
+            for i in range(2):
+                nc.vector.scalar_tensor_tensor(
+                    u_round[a][:, i * HALF : (i + 1) * HALF].rearrange("p (m t) -> p m t", t=PACK),
+                    u_diff[a, i][:].rearrange("p (m t) -> p m t", t=PACK),
+                    fk_col[:, a : a + 1],
+                    ra_all[:, :, i * 64 : (i + 1) * 64].rearrange("p t m -> p m t"),
+                    MULT,
+                    MULT,
+                )
+
+        def u_turn(a, bank):
+            words = u_round[a][:].bitcast(F32)
+            for half in range(2):
+                nc.tensor.transpose(bank[:, half, :], words[:, half : J // 2 : 2], ident[:])
+
+        def u_pack(name, bank, tiles, slot):
+            u_packed[name] = keep.tile([P, tiles * J], BF16, name=f"u_packed{name}", tag=slot, align_bytes=64)
+            nc.scalar.copy(
+                u_packed[name][:].bitcast(F32).rearrange("p (a m h) -> p a m h", a=tiles, h=2),
+                bank[:].rearrange("p a h m -> p a m h"),
+            )
+
+        def u_quantize(name, tiles):
+            codes = keep.tile([P, len(tiles) * P], U32, name=f"u_codes{name}", align_bytes=64)
+            plane = keep.tile([P, len(tiles) * P], U8, name=f"u_plane{name}", align_bytes=64)
+            nc.vector.quantize_mx(codes[:].bitcast(E4M3), plane[:], u_packed[name][:])
+            for i, a in enumerate(tiles):
+                u_codes[a] = codes[:, i * P : (i + 1) * P]
+                u_plane[a] = plane[:, i * P : (i + 1) * P]
+
+        def moment(a, b):
+            nc.tensor.matmul_mx(
+                out=w_bank[b][:, a, :],
+                lhsT=u_codes[a].bitcast(E4M3), lhsT_scale=u_plane[a],
+                rhs=g_codes[b][:].bitcast(E5M2), rhs_scale=g_plane[b][:],
+                start=True, stop=True,
+            )
+
+        bank01 = psum.tile([P, 2, 2, P], F32)
+        bank2 = psum.tile([P, 1, 2, P], F32)
+        bank3 = psum.tile([P, 1, 2, P], F32)
+
+        g_gather_first_vector(0)
+        g_gather_second(0)
+        g_turn(0)
+        u_gather_second(0)
+        u_gather_first(0)
+        u_scale(0)
+        u_turn(0, bank01[:, 0])
+        u_gather_second(1)
+        u_gather_first(1)
+        g_pack(0, "u_second10")
+        u_scale(1)
+        g_quantize(0)
+        g_gather_first_scalar(1)
+        g_gather_second(1)
+        g_turn(1)
+        u_turn(1, bank01[:, 1])
+        u_gather_second(2)
+        u_gather_first(2)
+        u_scale(2)
+        u_turn(2, bank2[:, 0])
+        u_gather_second(3)
+        u_gather_first(3)
+        u_scale(3)
+        u_turn(3, bank3[:, 0])
+        u_pack("01", bank01, 2, "u_second30")
+        u_pack("2", bank2, 1, "u_second31")
+        u_pack("3", bank3, 1, "u_packed3")
+        g_pack(1, "u_diff30")
+        u_quantize("01", (0, 1))
+        g_quantize(1)
+        u_quantize("2", (2,))
+        u_quantize("3", (3,))
+        for a, b in ((0, 0), (1, 0), (0, 1), (1, 1), (2, 0), (2, 1), (3, 0), (3, 1)):
+            moment(a, b)
+
+        w_packed = [keep.tile([P, K], BF16, name=f"w_packed{b}", align_bytes=64) for b in range(2)]
+        w_codes = [keep.tile([P, P], U32, name=f"w_codes{b}", align_bytes=64) for b in range(2)]
+        w_plane = [keep.tile([P, P], U8, name=f"w_plane{b}", align_bytes=64) for b in range(2)]
+        nc.scalar.copy(
+            w_packed[0][:].rearrange("p (m a) -> p m a", a=PACK), w_bank[0][:].rearrange("p a m -> p m a")
+        )
+        nc.vector.tensor_copy(
+            w_packed[1][:].rearrange("p (m a) -> p m a", a=PACK), w_bank[1][:].rearrange("p a m -> p m a")
+        )
+        for b in range(2):
+            nc.vector.quantize_mx(w_codes[b][:].bitcast(E5M2), w_plane[b][:], w_packed[b][:])
+
+        sums = keep.tile([P, 2, Q], F32)
+        result = keep.tile([P, 2, Q], F32)
+        v_bank = [psum.tile([P, P], F32, name=f"v_bank{h}", tag=f"g_bank{h}") for h in range(2)]
+        for b in range(2):
+            for h in range(2):
+                nc.tensor.matmul_mx(
+                    out=v_bank[h][:],
+                    lhsT=dr_codes[:, h * P : (h + 1) * P].bitcast(E4M3),
+                    lhsT_scale=dr_plane[:, h * P : (h + 1) * P],
+                    rhs=w_codes[b][:].bitcast(E5M2), rhs_scale=w_plane[b][:],
+                    start=(b == 0), stop=(b == 1),
+                )
+        for h in range(2):
+            nc.vector.tensor_reduce(
+                sums[:, h, :], v_bank[h][:].rearrange("p (q e) -> p q e", e=2), mybir.AxisListType.X, ADD
+            )
+        for h in range(2):
+            nc.vector.tensor_scalar(result[:, h, :], sums[:, h, :], gr_col[:, h : h + 1], 0.02, MULT, MULT)
+        nc.sync.dma_start(out=out.rearrange("(h p) q -> p h q", p=P), in_=result[:])

@@ -69,6 +69,11 @@ def tile_list_directions_gaps_differences_sums_kernel(
         with nc.allow_non_contiguous_dma(reason="one factor a partition"):
             nc.sync.dma_start(out=gr_col[:], in_=gr1c.rearrange("(h p) o -> p (h o)", p=P))
 
+        warm_in = keep.tile([P, 1], F32)
+        warm_out = keep.tile([P, 1], F32)
+        nc.vector.memset(warm_in[:], 0.0)
+        nc.scalar.activation(warm_out[:], warm_in[:], COPY)
+
         make_identity(nc, ident[:])
 
         ra_all = psum.tile([P, PACK, P], F32)

@@ -54,8 +54,8 @@ def tile_list_directions_gaps_differences_sums_kernel(
         nc.scalar.dma_start(out=fk_col[:], in_=fkr.rearrange("o (p a) -> p (o a)", a=PACK))
         nc.sync.dma_start(out=x_win[1][:], in_=x_rows[:, 1, :])
         nc.sync.dma_start(out=rb_col[:], in_=rb.rearrange("o (p t) -> p (o t)", t=PACK))
-        nc.sync.dma_start(out=g_win[1][:], in_=g_rows[:, 1, :])
         nc.sync.dma_start(out=x_win[2][:], in_=x_rows[:, 2, :])
+        nc.sync.dma_start(out=g_win[1][:], in_=g_rows[:, 1, :])
         nc.sync.dma_start(out=x_win[3][:], in_=x_rows[:, 3, :])
         nc.sync.dma_start(
             out=dr_codes[:].bitcast(I32), in_=dr_words[0].rearrange("p c t -> p (c t)").bitcast(I32)
@@ -119,19 +119,27 @@ def tile_list_directions_gaps_differences_sums_kernel(
             g_plane[b] = keep.tile([P, P], U8, name=f"g_plane{b}", align_bytes=64)
             nc.vector.quantize_mx(g_codes[b][:].bitcast(E5M2), g_plane[b][:], g_packed[b][:])
 
-        def u_gather_second(a):
-            for i in range(2):
-                u_second[a, i] = keep.tile([P, HALF], F32, name=f"u_second{a}{i}", align_bytes=64)
+        def u_gather_second(a, pieces=2):
+            cols = J // pieces
+            for i in range(pieces):
+                u_second[a, i] = keep.tile([P, cols], F32, name=f"u_second{a}{i}", align_bytes=64)
                 nc.scalar.activation(
-                    u_second[a, i][:], x_win[a][:].indirect(lists[1][:, i * 16 : (i + 1) * 16]), COPY
+                    u_second[a, i][:],
+                    x_win[a][:].indirect(lists[1][:, i * cols // 16 : (i + 1) * cols // 16]),
+                    COPY,
                 )
 
-        def u_gather_first(a):
-            for i in range(2):
-                u_diff[a, i] = keep.tile([P, HALF], F32, name=f"u_diff{a}{i}", align_bytes=64)
+        def u_gather_first(a, pieces=2):
+            cols = J // pieces
+            for half in range(2):
+                u_diff[a, half] = keep.tile([P, HALF], F32, name=f"u_diff{a}{half}", align_bytes=64)
+            for i in range(pieces):
+                half, start = divmod(i * cols, HALF)
                 nc.vector.tensor_tensor(
-                    u_diff[a, i][:], x_win[a][:].indirect(lists[0][:, i * 16 : (i + 1) * 16]),
-                    u_second[a, i][:], SUB,
+                    u_diff[a, half][:, start : start + cols],
+                    x_win[a][:].indirect(lists[0][:, i * cols // 16 : (i + 1) * cols // 16]),
+                    u_second[a, i][:],
+                    SUB,
                 )
 
         def u_scale(a):
@@ -181,8 +189,8 @@ def tile_list_directions_gaps_differences_sums_kernel(
         g_gather_first_vector(0)
         g_gather_second(0)
         g_turn(0)
-        u_gather_second(0)
-        u_gather_first(0)
+        u_gather_second(0, pieces=4)
+        u_gather_first(0, pieces=4)
         u_scale(0)
         u_turn(0, bank01[:, 0])
         u_gather_second(1)
@@ -190,11 +198,11 @@ def tile_list_directions_gaps_differences_sums_kernel(
         g_pack(0, "u_second10")
         u_scale(1)
         g_quantize(0)
+        u_turn(1, bank01[:, 1])
+        u_gather_second(2)
         g_gather_first_scalar(1)
         g_gather_second(1)
         g_turn(1)
-        u_turn(1, bank01[:, 1])
-        u_gather_second(2)
         u_gather_first(2)
         u_scale(2)
         u_turn(2, bank2[:, 0])

@@ -45,15 +45,15 @@ def tile_list_directions_gaps_differences_sums_kernel(
         ident = keep.tile([P, P], F32)
 
         nc.sync.dma_start(out=g_win[0][:], in_=g_rows[:, 0, :])
-        nc.sync.dma_start(lists[2][:], offs3)
         nc.sync.dma_start(lists[3][:], offs4)
+        nc.sync.dma_start(lists[2][:], offs3)
+        nc.scalar.dma_start(out=rb_col[:], in_=rb.rearrange("o (p t) -> p (o t)", t=PACK))
+        nc.scalar.dma_start(out=ra_col[:], in_=ra.rearrange("o (p t) -> p (o t)", t=PACK))
         nc.sync.dma_start(out=x_win[0][:], in_=x_rows[:, 0, :])
         nc.sync.dma_start(lists[1][:], offs2)
         nc.sync.dma_start(lists[0][:], offs)
-        nc.scalar.dma_start(out=ra_col[:], in_=ra.rearrange("o (p t) -> p (o t)", t=PACK))
-        nc.scalar.dma_start(out=fk_col[:], in_=fkr.rearrange("o (p a) -> p (o a)", a=PACK))
         nc.sync.dma_start(out=x_win[1][:], in_=x_rows[:, 1, :])
-        nc.sync.dma_start(out=rb_col[:], in_=rb.rearrange("o (p t) -> p (o t)", t=PACK))
+        nc.sync.dma_start(out=fk_col[:], in_=fkr.rearrange("o (p a) -> p (o a)", a=PACK))
         nc.sync.dma_start(out=x_win[2][:], in_=x_rows[:, 2, :])
         nc.sync.dma_start(out=g_win[1][:], in_=g_rows[:, 1, :])
         nc.sync.dma_start(out=x_win[3][:], in_=x_rows[:, 3, :])
@@ -76,150 +76,134 @@ def tile_list_directions_gaps_differences_sums_kernel(
 
         make_identity(nc, ident[:])
 
-        ra_all = psum.tile([P, PACK, P], F32)
-        for t in range(PACK):
-            nc.tensor.transpose(ra_all[:, t, :], ra_col[:, t : t + 1].to_broadcast([P, P]), ident[:])
+        ra_all = psum.tile([P, P, PACK], F32)
+        rb_all = psum.tile([P, P, PACK], F32)
+        for col, spread in ((rb_col, rb_all), (ra_col, ra_all)):
+            for t in range(PACK):
+                nc.tensor.transpose(spread[:, :, t], col[:, t : t + 1].to_broadcast([P, P]), ident[:])
 
         HALF = J // 2
-        u_second, u_diff, u_round, u_bank, u_packed, u_codes, u_plane = {}, {}, {}, {}, {}, {}, {}
-        g_packed, g_codes, g_plane = {}, {}, {}
-        g_first = [keep.tile([P, J], F32, name=f"g_first{b}") for b in range(2)]
-        g_second = [keep.tile([P, J], F32, name=f"g_second{b}") for b in range(2)]
-        g_bank = [psum.tile([P, PACK, P], F32, name=f"g_bank{b}") for b in range(2)]
+        second, diff, rounded, packed, codes, plane = {}, {}, {}, {}, {}, {}
+        window = {"g0": g_win[0], "g1": g_win[1], "u0": x_win[0], "u1": x_win[1], "u2": x_win[2], "u3": x_win[3]}
         w_bank = [psum.tile([P, PACK, P], F32, name=f"w_bank{b}") for b in range(2)]
 
-        def g_gather_first_vector(b):
-            nc.vector.tensor_copy(g_first[b][:], g_win[b][:].indirect(lists[2][:]))
-
-        def g_gather_first_scalar(b):
-            nc.scalar.activation(g_first[b][:], g_win[b][:].indirect(lists[2][:]), COPY)
-
-        def g_gather_second(b):
-            nc.scalar.activation(g_second[b][:], g_win[b][:].indirect(lists[3][:]), COPY, scale=-0.7)
-
-        def g_turn(b):
-            for i, picked in enumerate((g_first[b], g_second[b])):
-                for t in range(PACK):
-                    nc.tensor.matmul(
-                        g_bank[b][:, t, :], picked[:, t:J:PACK], ident[:], is_transpose=True,
-                        start=(i == 0 and t == 0), stop=(i == 1 and t == PACK - 1),
-                    )
-
-        def g_pack(b, slot):
-            g_packed[b] = keep.tile([P, J], BF16, name=f"g_packed{b}", tag=slot, align_bytes=64)
-            nc.vector.tensor_tensor(
-                g_packed[b][:].rearrange("p (m t) -> p m t", t=PACK),
-                g_bank[b][:].rearrange("p t m -> p m t"),
-                rb_col[:].unsqueeze(1).to_broadcast([P, P, PACK]),
-                MULT,
-            )
-
-        def g_quantize(b):
-            g_codes[b] = keep.tile([P, P], U32, name=f"g_codes{b}", align_bytes=64)
-            g_plane[b] = keep.tile([P, P], U8, name=f"g_plane{b}", align_bytes=64)
-            nc.vector.quantize_mx(g_codes[b][:].bitcast(E5M2), g_plane[b][:], g_packed[b][:])
-
-        def u_gather_second(a, pieces=2):
+        def gather_second(name, pieces):
             cols = J // pieces
+            offsets, factor = (lists[3], 0.7) if name[0] == "g" else (lists[1], 1.0)
             for i in range(pieces):
-                u_second[a, i] = keep.tile([P, cols], F32, name=f"u_second{a}{i}", align_bytes=64)
+                second[name, i] = keep.tile([P, cols], F32, name=f"second_{name}{i}", align_bytes=64)
                 nc.scalar.activation(
-                    u_second[a, i][:],
-                    x_win[a][:].indirect(lists[1][:, i * cols // 16 : (i + 1) * cols // 16]),
+                    second[name, i][:],
+                    window[name][:].indirect(offsets[:, i * cols // 16 : (i + 1) * cols // 16]),
                     COPY,
+                    scale=factor,
                 )
 
-        def u_gather_first(a, pieces=2):
+        def gather_first(name, pieces):
             cols = J // pieces
+            offsets = lists[2] if name[0] == "g" else lists[0]
             for half in range(2):
-                u_diff[a, half] = keep.tile([P, HALF], F32, name=f"u_diff{a}{half}", align_bytes=64)
+                diff[name, half] = keep.tile([P, HALF], F32, name=f"diff_{name}{half}", align_bytes=64)
             for i in range(pieces):
                 half, start = divmod(i * cols, HALF)
                 nc.vector.tensor_tensor(
-                    u_diff[a, half][:, start : start + cols],
-                    x_win[a][:].indirect(lists[0][:, i * cols // 16 : (i + 1) * cols // 16]),
-                    u_second[a, i][:],
+                    diff[name, half][:, start : start + cols],
+                    window[name][:].indirect(offsets[:, i * cols // 16 : (i + 1) * cols // 16]),
+                    second[name, i][:],
                     SUB,
                 )
 
-        def u_scale(a):
-            u_round[a] = keep.tile([P, J], BF16, name=f"u_round{a}")
+        def weigh(name):
+            rounded[name] = keep.tile([P, J], BF16, name=f"rounded_{name}")
             for i in range(2):
-                nc.vector.scalar_tensor_tensor(
-                    u_round[a][:, i * HALF : (i + 1) * HALF].rearrange("p (m t) -> p m t", t=PACK),
-                    u_diff[a, i][:].rearrange("p (m t) -> p m t", t=PACK),
-                    fk_col[:, a : a + 1],
-                    ra_all[:, :, i * 64 : (i + 1) * 64].rearrange("p t m -> p m t"),
-                    MULT,
-                    MULT,
-                )
+                cols = slice(i * HALF, (i + 1) * HALF)
+                if name[0] == "g":
+                    nc.vector.tensor_tensor(
+                        rounded[name][:, cols], diff[name, i][:],
+                        rb_all[:].rearrange("p m t -> p (m t)")[:, cols], MULT,
+                    )
+                else:
+                    a = int(name[1])
+                    nc.vector.scalar_tensor_tensor(
+                        rounded[name][:, cols], diff[name, i][:], fk_col[:, a : a + 1],
+                        ra_all[:].rearrange("p m t -> p (m t)")[:, cols], MULT, MULT,
+                    )
 
-        def u_turn(a, bank):
-            words = u_round[a][:].bitcast(F32)
+        def turn(name, bank):
+            words = rounded[name][:].bitcast(F32)
             for half in range(2):
                 nc.tensor.transpose(bank[:, half, :], words[:, half : J // 2 : 2], ident[:])
 
-        def u_pack(name, bank, tiles, slot):
-            u_packed[name] = keep.tile([P, tiles * J], BF16, name=f"u_packed{name}", tag=slot, align_bytes=64)
+        def pack(names, bank, slot):
+            tile = keep.tile([P, len(names) * J], BF16, name="packed_" + names[0], tag=slot, align_bytes=64)
             nc.scalar.copy(
-                u_packed[name][:].bitcast(F32).rearrange("p (a m h) -> p a m h", a=tiles, h=2),
+                tile[:].bitcast(F32).rearrange("p (a m h) -> p a m h", a=len(names), h=2),
                 bank[:].rearrange("p a h m -> p a m h"),
             )
+            return tile
 
-        def u_quantize(name, tiles):
-            codes = keep.tile([P, len(tiles) * P], U32, name=f"u_codes{name}", align_bytes=64)
-            plane = keep.tile([P, len(tiles) * P], U8, name=f"u_plane{name}", align_bytes=64)
-            nc.vector.quantize_mx(codes[:].bitcast(E4M3), plane[:], u_packed[name][:])
-            for i, a in enumerate(tiles):
-                u_codes[a] = codes[:, i * P : (i + 1) * P]
-                u_plane[a] = plane[:, i * P : (i + 1) * P]
+        def quantize(names, source, fmt):
+            words = keep.tile([P, len(names) * P], U32, name="codes_" + names[0], align_bytes=64)
+            scales = keep.tile([P, len(names) * P], U8, name="plane_" + names[0], align_bytes=64)
+            nc.vector.quantize_mx(words[:].bitcast(fmt), scales[:], source)
+            for i, name in enumerate(names):
+                codes[name] = words[:, i * P : (i + 1) * P].bitcast(fmt)
+                plane[name] = scales[:, i * P : (i + 1) * P]
 
         def moment(a, b):
             nc.tensor.matmul_mx(
                 out=w_bank[b][:, a, :],
-                lhsT=u_codes[a].bitcast(E4M3), lhsT_scale=u_plane[a],
-                rhs=g_codes[b][:].bitcast(E5M2), rhs_scale=g_plane[b][:],
+                lhsT=codes[f"u{a}"], lhsT_scale=plane[f"u{a}"],
+                rhs=codes[f"g{b}"], rhs_scale=plane[f"g{b}"],
                 start=True, stop=True,
             )
 
-        bank01 = psum.tile([P, 2, 2, P], F32)
-        bank2 = psum.tile([P, 1, 2, P], F32)
-        bank3 = psum.tile([P, 1, 2, P], F32)
+        bank_a = psum.tile([P, 2, 2, P], F32)
+        bank_b = psum.tile([P, 2, 2, P], F32)
+        bank_c = psum.tile([P, 1, 2, P], F32)
+        g_bank = psum.tile([P, PACK, P], F32)
+        g_first = keep.tile([P, J], F32)
+        g_second = keep.tile([P, J], F32)
 
-        g_gather_first_vector(0)
-        g_gather_second(0)
-        g_turn(0)
-        u_gather_second(0, pieces=4)
-        u_gather_first(0, pieces=4)
-        u_scale(0)
-        u_turn(0, bank01[:, 0])
-        u_gather_second(1)
-        u_gather_first(1)
-        g_pack(0, "u_second10")
-        u_scale(1)
-        g_quantize(0)
-        u_turn(1, bank01[:, 1])
-        u_gather_second(2)
-        g_gather_first_scalar(1)
-        g_gather_second(1)
-        g_turn(1)
-        u_gather_first(2)
-        u_scale(2)
-        u_turn(2, bank2[:, 0])
-        u_gather_second(3)
-        u_gather_first(3)
-        u_scale(3)
-        u_turn(3, bank3[:, 0])
-        u_pack("01", bank01, 2, "u_second30")
-        u_pack("2", bank2, 1, "u_second31")
-        u_pack("3", bank3, 1, "u_packed3")
-        g_pack(1, "u_diff30")
-        u_quantize("01", (0, 1))
-        g_quantize(1)
-        u_quantize("2", (2,))
-        u_quantize("3", (3,))
-        for a, b in ((0, 0), (1, 0), (0, 1), (1, 1), (2, 0), (2, 1), (3, 0), (3, 1)):
-            moment(a, b)
+        for name, bank, pieces in (("g0", bank_a[:, 0], 4), ("u0", bank_a[:, 1], 2), ("u1", bank_b[:, 0], 2)):
+            gather_second(name, pieces)
+            gather_first(name, pieces)
+            weigh(name)
+            turn(name, bank)
+        gather_second("u2", 2)
+        nc.scalar.activation(g_first[:], g_win[1][:].indirect(lists[2][:]), COPY)
+        nc.scalar.activation(g_second[:], g_win[1][:].indirect(lists[3][:]), COPY, scale=-0.7)
+        for i, picked in enumerate((g_first, g_second)):
+            for t in range(PACK):
+                nc.tensor.matmul(
+                    g_bank[:, t, :], picked[:, t:J:PACK], ident[:], is_transpose=True,
+                    start=(i == 0 and t == 0), stop=(i == 1 and t == PACK - 1),
+                )
+        gather_first("u2", 2)
+        weigh("u2")
+        turn("u2", bank_b[:, 1])
+        gather_second("u3", 2)
+        gather_first("u3", 2)
+        weigh("u3")
+        turn("u3", bank_c[:, 0])
+        packed_a = pack(("g0", "u0"), bank_a, "second_u30")
+        packed_b = pack(("u1", "u2"), bank_b, "second_u31")
+        packed_c = pack(("u3",), bank_c, "packed_u3")
+        g_packed = keep.tile([P, J], BF16, tag="diff_u30", align_bytes=64)
+        nc.vector.tensor_tensor(
+            g_packed[:].rearrange("p (m t) -> p m t", t=PACK),
+            g_bank[:].rearrange("p t m -> p m t"),
+            rb_col[:].unsqueeze(1).to_broadcast([P, P, PACK]),
+            MULT,
+        )
+        quantize(("g0",), packed_a[:, 0:J], E5M2)
+        quantize(("u0",), packed_a[:, J : 2 * J], E4M3)
+        quantize(("g1",), g_packed[:], E5M2)
+        quantize(("u1", "u2"), packed_b[:], E4M3)
+        quantize(("u3",), packed_c[:], E4M3)
+        for a in range(PACK):
+            for b in range(2):
+                moment(a, b)
 
         w_packed = [keep.tile([P, K], BF16, name=f"w_packed{b}", align_bytes=64) for b in range(2)]
         w_codes = [keep.tile([P, P], U32, name=f"w_codes{b}", align_bytes=64) for b in range(2)]
@@ -235,7 +219,7 @@ def tile_list_directions_gaps_differences_sums_kernel(
 
         sums = keep.tile([P, 2, Q], F32)
         result = keep.tile([P, 2, Q], F32)
-        v_bank = [psum.tile([P, P], F32, name=f"v_bank{h}", tag=f"g_bank{h}") for h in range(2)]
+        v_bank = [psum.tile([P, P], F32, name=f"v_bank{h}", tag=("ra_all", "rb_all")[h]) for h in range(2)]
         for b in range(2):
             for h in range(2):
                 nc.tensor.matmul_mx(

from contextlib import ExitStack

import concourse.mybir as mybir
from concourse.masks import make_identity

K, J, N, R, T, V, Q = 512, 512, 256, 256, 1024, 1024, 64
FLOPS = 2 * J * K * N + 2 * K * R * N

F32 = mybir.dt.float32
BF16 = mybir.dt.bfloat16
I32 = mybir.dt.int32
U32 = mybir.dt.uint32
U16 = mybir.dt.uint16
U8 = mybir.dt.uint8
E4M3 = mybir.dt.float8_e4m3fn_x4
E5M2 = mybir.dt.float8_e5m2_x4
MULT = mybir.AluOpType.mult
ADD = mybir.AluOpType.add
SUB = mybir.AluOpType.subtract
COPY = mybir.ActivationFunctionType.Copy

P = 128
PACK = 4


def tile_list_directions_gaps_differences_sums_kernel(
    tc, xf, ra, gt, rb, fkr, dr_words, dr_scales, gr1c, offs, offs2, offs3, offs4, out
):
    nc = tc.nc
    with ExitStack() as ctx:
        keep = ctx.enter_context(tc.tile_pool(name="keep", bufs=1))
        psum = ctx.enter_context(tc.psum_pool(name="psum", bufs=1))

        lists = [keep.tile([P, J // 16], U16, name=f"list{i}") for i in range(4)]
        x_rows = xf.rearrange("(p a) t -> p a t", a=PACK)
        g_rows = gt.rearrange("(p b) v -> p b v", b=2)
        x_win = [keep.tile([P, T], F32, name=f"x_win{a}") for a in range(PACK)]
        g_win = [keep.tile([P, V], F32, name=f"g_win{b}") for b in range(2)]
        ra_col = keep.tile([P, PACK], F32)
        rb_col = keep.tile([P, PACK], F32)
        fk_col = keep.tile([P, PACK], F32)
        gr_col = keep.tile([P, 2], F32)
        dr_codes = keep.tile([P, R], U32, align_bytes=64)
        dr_plane = keep.tile([P, R], U8, align_bytes=64)
        ident = keep.tile([P, P], F32)

        nc.sync.dma_start(out=g_win[0][:], in_=g_rows[:, 0, :])
        nc.sync.dma_start(lists[3][:], offs4)
        nc.sync.dma_start(lists[2][:], offs3)
        nc.scalar.dma_start(out=rb_col[:], in_=rb.rearrange("o (p t) -> p (o t)", t=PACK))
        nc.scalar.dma_start(out=ra_col[:], in_=ra.rearrange("o (p t) -> p (o t)", t=PACK))
        nc.sync.dma_start(out=x_win[0][:], in_=x_rows[:, 0, :])
        nc.sync.dma_start(lists[1][:], offs2)
        nc.sync.dma_start(lists[0][:], offs)
        nc.sync.dma_start(out=x_win[1][:], in_=x_rows[:, 1, :])
        nc.sync.dma_start(out=fk_col[:], in_=fkr.rearrange("o (p a) -> p (o a)", a=PACK))
        nc.sync.dma_start(out=x_win[2][:], in_=x_rows[:, 2, :])
        nc.sync.dma_start(out=g_win[1][:], in_=g_rows[:, 1, :])
        nc.sync.dma_start(out=x_win[3][:], in_=x_rows[:, 3, :])
        nc.sync.dma_start(
            out=dr_codes[:].bitcast(I32), in_=dr_words[0].rearrange("p c t -> p (c t)").bitcast(I32)
        )
        nc.gpsimd.memset(dr_plane[:].bitcast(I32), 0)
        for quad in range(4):
            nc.sync.dma_start(
                out=dr_plane[32 * quad : 32 * quad + 4, :].bitcast(I32),
                in_=dr_scales[0, 4 * quad : 4 * quad + 4, :].bitcast(I32),
            )
        with nc.allow_non_contiguous_dma(reason="one factor a partition"):
            nc.sync.dma_start(out=gr_col[:], in_=gr1c.rearrange("(h p) o -> p (h o)", p=P))

        warm_in = keep.tile([P, 1], F32)
        warm_out = keep.tile([P, 1], F32)
        nc.vector.memset(warm_in[:], 0.0)
        nc.scalar.activation(warm_out[:], warm_in[:], COPY)

        make_identity(nc, ident[:])

        ra_all = psum.tile([P, P, PACK], F32)
        rb_all = psum.tile([P, P, PACK], F32)
        for col, spread in ((rb_col, rb_all), (ra_col, ra_all)):
            for t in range(PACK):
                nc.tensor.transpose(spread[:, :, t], col[:, t : t + 1].to_broadcast([P, P]), ident[:])

        HALF = J // 2
        second, diff, rounded, packed, codes, plane = {}, {}, {}, {}, {}, {}
        window = {"g0": g_win[0], "g1": g_win[1], "u0": x_win[0], "u1": x_win[1], "u2": x_win[2], "u3": x_win[3]}
        w_bank = [psum.tile([P, PACK, P], F32, name=f"w_bank{b}") for b in range(2)]

        def gather_second(name, pieces):
            cols = J // pieces
            offsets, factor = (lists[3], 0.7) if name[0] == "g" else (lists[1], 1.0)
            for i in range(pieces):
                second[name, i] = keep.tile([P, cols], F32, name=f"second_{name}{i}", align_bytes=64)
                nc.scalar.activation(
                    second[name, i][:],
                    window[name][:].indirect(offsets[:, i * cols // 16 : (i + 1) * cols // 16]),
                    COPY,
                    scale=factor,
                )

        def gather_first(name, pieces):
            cols = J // pieces
            offsets = lists[2] if name[0] == "g" else lists[0]
            for half in range(2):
                diff[name, half] = keep.tile([P, HALF], F32, name=f"diff_{name}{half}", align_bytes=64)
            for i in range(pieces):
                half, start = divmod(i * cols, HALF)
                nc.vector.tensor_tensor(
                    diff[name, half][:, start : start + cols],
                    window[name][:].indirect(offsets[:, i * cols // 16 : (i + 1) * cols // 16]),
                    second[name, i][:],
                    SUB,
                )

        def weigh(name):
            rounded[name] = keep.tile([P, J], BF16, name=f"rounded_{name}")
            for i in range(2):
                cols = slice(i * HALF, (i + 1) * HALF)
                if name[0] == "g":
                    nc.vector.tensor_tensor(
                        rounded[name][:, cols], diff[name, i][:],
                        rb_all[:].rearrange("p m t -> p (m t)")[:, cols], MULT,
                    )
                else:
                    a = int(name[1])
                    nc.vector.scalar_tensor_tensor(
                        rounded[name][:, cols], diff[name, i][:], fk_col[:, a : a + 1],
                        ra_all[:].rearrange("p m t -> p (m t)")[:, cols], MULT, MULT,
                    )

        def turn(name, bank):
            words = rounded[name][:].bitcast(F32)
            for half in range(2):
                nc.tensor.transpose(bank[:, half, :], words[:, half : J // 2 : 2], ident[:])

        def pack(names, bank, slot):
            tile = keep.tile([P, len(names) * J], BF16, name="packed_" + names[0], tag=slot, align_bytes=64)
            nc.scalar.copy(
                tile[:].bitcast(F32).rearrange("p (a m h) -> p a m h", a=len(names), h=2),
                bank[:].rearrange("p a h m -> p a m h"),
            )
            return tile

        def quantize(names, source, fmt):
            words = keep.tile([P, len(names) * P], U32, name="codes_" + names[0], align_bytes=64)
            scales = keep.tile([P, len(names) * P], U8, name="plane_" + names[0], align_bytes=64)
            nc.vector.quantize_mx(words[:].bitcast(fmt), scales[:], source)
            for i, name in enumerate(names):
                codes[name] = words[:, i * P : (i + 1) * P].bitcast(fmt)
                plane[name] = scales[:, i * P : (i + 1) * P]

        def moment(a, b):
            nc.tensor.matmul_mx(
                out=w_bank[b][:, a, :],
                lhsT=codes[f"u{a}"], lhsT_scale=plane[f"u{a}"],
                rhs=codes[f"g{b}"], rhs_scale=plane[f"g{b}"],
                start=True, stop=True,
            )

        bank_a = psum.tile([P, 2, 2, P], F32)
        bank_b = psum.tile([P, 2, 2, P], F32)
        bank_c = psum.tile([P, 1, 2, P], F32)
        g_bank = psum.tile([P, PACK, P], F32)
        g_first = keep.tile([P, J], F32)
        g_second = keep.tile([P, J], F32)

        for name, bank, pieces in (("g0", bank_a[:, 0], 4), ("u0", bank_a[:, 1], 2), ("u1", bank_b[:, 0], 2)):
            gather_second(name, pieces)
            gather_first(name, pieces)
            weigh(name)
            turn(name, bank)
        gather_second("u2", 2)
        nc.scalar.activation(g_first[:], g_win[1][:].indirect(lists[2][:]), COPY)
        nc.scalar.activation(g_second[:], g_win[1][:].indirect(lists[3][:]), COPY, scale=-0.7)
        for i, picked in enumerate((g_first, g_second)):
            for t in range(PACK):
                nc.tensor.matmul(
                    g_bank[:, t, :], picked[:, t:J:PACK], ident[:], is_transpose=True,
                    start=(i == 0 and t == 0), stop=(i == 1 and t == PACK - 1),
                )
        gather_first("u2", 2)
        weigh("u2")
        turn("u2", bank_b[:, 1])
        gather_second("u3", 2)
        gather_first("u3", 2)
        weigh("u3")
        turn("u3", bank_c[:, 0])
        packed_a = pack(("g0", "u0"), bank_a, "second_u30")
        packed_b = pack(("u1", "u2"), bank_b, "second_u31")
        packed_c = pack(("u3",), bank_c, "packed_u3")
        g_packed = keep.tile([P, J], BF16, tag="diff_u30", align_bytes=64)
        nc.vector.tensor_tensor(
            g_packed[:].rearrange("p (m t) -> p m t", t=PACK),
            g_bank[:].rearrange("p t m -> p m t"),
            rb_col[:].unsqueeze(1).to_broadcast([P, P, PACK]),
            MULT,
        )
        quantize(("g0",), packed_a[:, 0:J], E5M2)
        quantize(("u0",), packed_a[:, J : 2 * J], E4M3)
        quantize(("g1",), g_packed[:], E5M2)
        quantize(("u1", "u2"), packed_b[:], E4M3)
        quantize(("u3",), packed_c[:], E4M3)
        for a in range(PACK):
            for b in range(2):
                moment(a, b)

        w_packed = [keep.tile([P, K], BF16, name=f"w_packed{b}", align_bytes=64) for b in range(2)]
        w_codes = [keep.tile([P, P], U32, name=f"w_codes{b}", align_bytes=64) for b in range(2)]
        w_plane = [keep.tile([P, P], U8, name=f"w_plane{b}", align_bytes=64) for b in range(2)]
        nc.scalar.copy(
            w_packed[0][:].rearrange("p (m a) -> p m a", a=PACK), w_bank[0][:].rearrange("p a m -> p m a")
        )
        nc.vector.tensor_copy(
            w_packed[1][:].rearrange("p (m a) -> p m a", a=PACK), w_bank[1][:].rearrange("p a m -> p m a")
        )
        for b in range(2):
            nc.vector.quantize_mx(w_codes[b][:].bitcast(E5M2), w_plane[b][:], w_packed[b][:])

        sums = keep.tile([P, 2, Q], F32)
        result = keep.tile([P, 2, Q], F32)
        v_bank = [psum.tile([P, P], F32, name=f"v_bank{h}", tag=("ra_all", "rb_all")[h]) for h in range(2)]
        for b in range(2):
            for h in range(2):
                nc.tensor.matmul_mx(
                    out=v_bank[h][:],
                    lhsT=dr_codes[:, h * P : (h + 1) * P].bitcast(E4M3),
                    lhsT_scale=dr_plane[:, h * P : (h + 1) * P],
                    rhs=w_codes[b][:].bitcast(E5M2), rhs_scale=w_plane[b][:],
                    start=(b == 0), stop=(b == 1),
                )
        for h in range(2):
            nc.vector.tensor_reduce(
                sums[:, h, :], v_bank[h][:].rearrange("p (q e) -> p q e", e=2), mybir.AxisListType.X, ADD
            )
        for h in range(2):
            nc.vector.tensor_scalar(result[:, h, :], sums[:, h, :], gr_col[:, h : h + 1], 0.02, MULT, MULT)
        nc.sync.dma_start(out=out.rearrange("(h p) q -> p h q", p=P), in_=result[:])
